import numpy as np
CORES = [10,50,90,98,138,178,218,226,266,306,346,354,394,434,474,482]
N = 16
ROUNDS, ROOT = 8, 9
def setup_inputs(rng):
    return {"x": rng.standard_normal((N, ROUNDS, 128, 128), dtype=np.float32)}
def reference(x):
    y = np.full(x.shape, np.nan, x.dtype)
    y[ROOT] = x.sum(axis=0, dtype=np.float64).astype(x.dtype)
    return {"y": y}

@@ -1,0 +1,76 @@
+from concourse.mybir import AluOpType
+
+HALF = 4
+COLS = HALF * 128
+SCRATCH = {
+    "buf": ("dram", [128, COLS], "float32"),
+}
+SEMAPHORES = ["dma", "inbox", "sent"]
+
+LINE_A = [(1, 6), (1, 12), (1, 11), (1, 1),
+          (0, 1), (0, 11), (0, 12), (0, 6),
+          (3, 6), (3, 12), (3, 11), (3, 1),
+          (2, 1), (2, 11), (2, 12), (2, 6)]
+LINE = [LINE_A, LINE_A]
+DATA, CREDIT = 8, 1
+
+
+def rank_program(g, core, T, topo):
+    if T.rank_of(core) is None:
+        return
+    sem = T.sem
+    lines = [[h * 128 + c * 8 + 2 for (h, c) in ln] for ln in LINE]
+    pos = [ln.index(core) for ln in lines]
+    prev = [ln[p - 1] if p > 0 else None for ln, p in zip(lines, pos)]
+    nxt = [ln[p + 1] if p + 1 < len(ln) else None for ln, p in zip(lines, pos)]
+    root = nxt[0] is None
+    n = {"dma": 0, "inbox": 0, "sent": 0}
+
+    def local(out, in_, add):
+        if add:
+            d = g.dma_start(out, in_, accum_op=AluOpType.add, max_dma_last_dim=8192)
+        else:
+            d = g.dma_start(out, in_)
+        d.then_inc(sem.dma, 16)
+        n["dma"] += 16
+        g.wait_ge(sem.dma, n["dma"])
+
+    def send(dst):
+        rid, pid = topo.addr(dst, core)
+        g.remote_dma(out_ap=T.buf[:], in_ap=T.buf[:], remote_sem=sem.inbox, local_sem=sem.sent,
+                     pid=pid, routing_id=rid, dma_engine_mask=topo.mask(core, dst))
+        n["sent"] += DATA
+
+    def credit(dst):
+        rid, pid = topo.addr(dst, core)
+        g.remote_sem_update(remote_sem=sem.inbox, local_sem=sem.sent, pid=pid, routing_id=rid, dma_engine_mask=0x01)
+        n["sent"] += CREDIT
+
+    def await_inbox(k):
+        if k:
+            n["inbox"] += k
+            g.wait_ge(sem.inbox, n["inbox"])
+
+    early = nxt[1] is not None and lines[0].index(nxt[1]) < pos[0]
+    late = nxt[1] is not None and not early
+
+    if root:
+        local(T.y[:], T.x[:], add=False)
+        await_inbox(DATA)
+        local(T.y[0:HALF], T.buf[:], add=True)
+        credit(prev[1])
+        await_inbox(DATA)
+        local(T.y[HALF:2 * HALF], T.buf[:], add=True)
+        g.wait_ge(sem.sent, n["sent"])
+        return
+
+    await_inbox((DATA if prev[0] is not None else 0) + (CREDIT if early else 0))
+    local(T.buf[:], T.x[0:HALF], add=prev[0] is not None)
+    send(nxt[0])
+    g.wait_ge(sem.sent, n["sent"])
+    if prev[1] is not None:
+        credit(prev[1])
+    await_inbox((DATA if prev[1] is not None else 0) + (CREDIT if late else 0))
+    local(T.buf[:], T.x[HALF:2 * HALF], add=prev[1] is not None)
+    send(nxt[1])
+    g.wait_ge(sem.sent, n["sent"])

@@ -11,7 +11,10 @@ LINE_A = [(1, 6), (1, 12), (1, 11), (1, 1),
           (0, 1), (0, 11), (0, 12), (0, 6),
           (3, 6), (3, 12), (3, 11), (3, 1),
           (2, 1), (2, 11), (2, 12), (2, 6)]
-LINE = [LINE_A, LINE_A]
+LINE_B = [(1, 12), (1, 6), (1, 1), (1, 11),
+          (0, 11), (0, 1), (0, 6), (0, 12),
+          (3, 12), (3, 6), (3, 1), (3, 11),
+          (2, 11), (2, 1), (2, 12), (2, 6)]
 DATA, CREDIT = 8, 1
 
 
@@ -19,12 +22,14 @@ def rank_program(g, core, T, topo):
     if T.rank_of(core) is None:
         return
     sem = T.sem
-    lines = [[h * 128 + c * 8 + 2 for (h, c) in ln] for ln in LINE]
+    lines = [[h * 128 + c * 8 + 2 for (h, c) in ln] for ln in (LINE_A, LINE_B)]
     pos = [ln.index(core) for ln in lines]
     prev = [ln[p - 1] if p > 0 else None for ln, p in zip(lines, pos)]
     nxt = [ln[p + 1] if p + 1 < len(ln) else None for ln, p in zip(lines, pos)]
-    root = nxt[0] is None
     n = {"dma": 0, "inbox": 0, "sent": 0}
+
+    def before(a, b):
+        return lines[0].index(a) < lines[0].index(b)
 
     def local(out, in_, add):
         if add:
@@ -43,7 +48,8 @@ def rank_program(g, core, T, topo):
 
     def credit(dst):
         rid, pid = topo.addr(dst, core)
-        g.remote_sem_update(remote_sem=sem.inbox, local_sem=sem.sent, pid=pid, routing_id=rid, dma_engine_mask=0x01)
+        g.remote_sem_update(remote_sem=sem.sent if before(core, dst) else sem.inbox, local_sem=sem.sent,
+                            pid=pid, routing_id=rid, dma_engine_mask=0x01)
         n["sent"] += CREDIT
 
     def await_inbox(k):
@@ -51,10 +57,7 @@ def rank_program(g, core, T, topo):
             n["inbox"] += k
             g.wait_ge(sem.inbox, n["inbox"])
 
-    early = nxt[1] is not None and lines[0].index(nxt[1]) < pos[0]
-    late = nxt[1] is not None and not early
-
-    if root:
+    if nxt[0] is None:
         local(T.y[:], T.x[:], add=False)
         await_inbox(DATA)
         local(T.y[0:HALF], T.buf[:], add=True)
@@ -64,13 +67,15 @@ def rank_program(g, core, T, topo):
         g.wait_ge(sem.sent, n["sent"])
         return
 
-    await_inbox((DATA if prev[0] is not None else 0) + (CREDIT if early else 0))
+    early = before(nxt[1], core)
+    await_inbox(DATA if prev[0] is not None else 0)
     local(T.buf[:], T.x[0:HALF], add=prev[0] is not None)
     send(nxt[0])
+    n["sent"] += CREDIT if early else 0
     g.wait_ge(sem.sent, n["sent"])
     if prev[1] is not None:
         credit(prev[1])
-    await_inbox((DATA if prev[1] is not None else 0) + (CREDIT if late else 0))
+    await_inbox((DATA if prev[1] is not None else 0) + (0 if early else CREDIT))
     local(T.buf[:], T.x[HALF:2 * HALF], add=prev[1] is not None)
     send(nxt[1])
     g.wait_ge(sem.sent, n["sent"])

from concourse.mybir import AluOpType

HALF = 4
COLS = HALF * 128
SCRATCH = {
    "buf": ("dram", [128, COLS], "float32"),
}
SEMAPHORES = ["dma", "inbox", "sent"]

LINE_A = [(1, 6), (1, 12), (1, 11), (1, 1),
          (0, 1), (0, 11), (0, 12), (0, 6),
          (3, 6), (3, 12), (3, 11), (3, 1),
          (2, 1), (2, 11), (2, 12), (2, 6)]
LINE_B = [(1, 12), (1, 6), (1, 1), (1, 11),
          (0, 11), (0, 1), (0, 6), (0, 12),
          (3, 12), (3, 6), (3, 1), (3, 11),
          (2, 11), (2, 1), (2, 12), (2, 6)]
DATA, CREDIT = 8, 1


def rank_program(g, core, T, topo):
    if T.rank_of(core) is None:
        return
    sem = T.sem
    lines = [[h * 128 + c * 8 + 2 for (h, c) in ln] for ln in (LINE_A, LINE_B)]
    pos = [ln.index(core) for ln in lines]
    prev = [ln[p - 1] if p > 0 else None for ln, p in zip(lines, pos)]
    nxt = [ln[p + 1] if p + 1 < len(ln) else None for ln, p in zip(lines, pos)]
    n = {"dma": 0, "inbox": 0, "sent": 0}

    def before(a, b):
        return lines[0].index(a) < lines[0].index(b)

    def local(out, in_, add):
        if add:
            d = g.dma_start(out, in_, accum_op=AluOpType.add, max_dma_last_dim=8192)
        else:
            d = g.dma_start(out, in_)
        d.then_inc(sem.dma, 16)
        n["dma"] += 16
        g.wait_ge(sem.dma, n["dma"])

    def send(dst):
        rid, pid = topo.addr(dst, core)
        g.remote_dma(out_ap=T.buf[:], in_ap=T.buf[:], remote_sem=sem.inbox, local_sem=sem.sent,
                     pid=pid, routing_id=rid, dma_engine_mask=topo.mask(core, dst))
        n["sent"] += DATA

    def credit(dst):
        rid, pid = topo.addr(dst, core)
        g.remote_sem_update(remote_sem=sem.sent if before(core, dst) else sem.inbox, local_sem=sem.sent,
                            pid=pid, routing_id=rid, dma_engine_mask=0x01)
        n["sent"] += CREDIT

    def await_inbox(k):
        if k:
            n["inbox"] += k
            g.wait_ge(sem.inbox, n["inbox"])

    if nxt[0] is None:
        local(T.y[:], T.x[:], add=False)
        await_inbox(DATA)
        local(T.y[0:HALF], T.buf[:], add=True)
        credit(prev[1])
        await_inbox(DATA)
        local(T.y[HALF:2 * HALF], T.buf[:], add=True)
        g.wait_ge(sem.sent, n["sent"])
        return

    early = before(nxt[1], core)
    await_inbox(DATA if prev[0] is not None else 0)
    local(T.buf[:], T.x[0:HALF], add=prev[0] is not None)
    send(nxt[0])
    n["sent"] += CREDIT if early else 0
    g.wait_ge(sem.sent, n["sent"])
    if prev[1] is not None:
        credit(prev[1])
    await_inbox((DATA if prev[1] is not None else 0) + (0 if early else CREDIT))
    local(T.buf[:], T.x[HALF:2 * HALF], add=prev[1] is not None)
    send(nxt[1])
    g.wait_ge(sem.sent, n["sent"])
